import numpy as np
import ml_dtypes


def mxq(x, axis, fmt="e4m3"):
    dtype, down = {"e4m3": (ml_dtypes.float8_e4m3fn, 7), "e5m2": (ml_dtypes.float8_e5m2, 14)}[fmt]
    v = np.moveaxis(np.asarray(x, np.float32).astype(ml_dtypes.bfloat16).astype(np.float64), axis, -1)
    blocks = v.reshape(v.shape[:-1] + (-1, 32))
    amax = np.abs(blocks).max(-1, keepdims=True)
    byte = np.maximum(np.where(amax > 0, np.frexp(amax)[1] - 1 + 127, 0) - down, 1)
    scale = np.exp2(byte - 127.0)
    codes = (blocks / scale).astype(np.float32).astype(dtype).astype(np.float64)
    return np.moveaxis((codes * scale).reshape(v.shape), -1, axis)


WIDE = False


def mx_kscale(k):
    if not WIDE:
        return np.ones(k)
    levels = np.array([10, -10, 5, -5, 0])
    if k % 512:
        return np.exp2(np.random.permutation(np.resize(levels, k // 32))).repeat(32)
    a = np.empty((k // 512, 16))
    for p in range(k // 512):
        a[p, :8] = np.random.permutation(np.resize(levels, 8))
        for g in range(8):
            far = levels[np.abs(levels - a[p, g]) >= 10]
            a[p, g + 8] = far[np.random.randint(len(far))]
    return np.exp2(a.ravel()).repeat(32)


def f64(x):
    return np.asarray(x).astype(np.float64)


def striped(idx):
    return np.tile(idx.reshape(-1, 16).T, (8, 1)).astype(np.uint16)


def unstriped(offs):
    return offs[:16].T.reshape(-1).astype(np.int64)


E2M1 = np.array([0.0, 0.5, 1.0, 1.5, 2.0, 3.0, 4.0, 6.0, -0.0, -0.5, -1.0, -1.5, -2.0, -3.0, -4.0, -6.0])


def pack_weight(w, fmt):
    k, n = w.shape
    w = f64(np.asarray(w, np.float32).astype(ml_dtypes.bfloat16)).reshape(k // 32, 32, n)
    amax = np.abs(w).max(1)
    if fmt == "e4m3":
        byte = np.frexp(amax)[1] - 1 + 127 - 7
    else:
        mant, ex = np.frexp(amax / 6.0)
        byte = np.where(mant > 0.5, ex, ex - 1) + 127
    byte = np.clip(np.where(amax > 0, byte, 1), 1, 254)
    scaled = (w * np.exp2(127.0 - byte)[:, None, :]).reshape(k, n).astype(np.float32)
    by_word = np.ascontiguousarray(scaled.reshape(k // 512, 128, 4, n).transpose(0, 1, 3, 2))
    if fmt == "e4m3":
        words = by_word.astype(ml_dtypes.float8_e4m3fn).view(np.uint8)
    else:
        c = by_word.astype(ml_dtypes.float4_e2m1fn).view(np.uint8) & 0xF
        words = (c[..., 0::2] | (c[..., 1::2] << 4)).reshape(k // 512, 128, 2 * n)
    return np.ascontiguousarray(words), np.ascontiguousarray(byte.astype(np.uint8).reshape(k // 512, 16, n))


def unpack_weight(words, scales, fmt):
    g, _, n = scales.shape
    words = np.ascontiguousarray(words).reshape(g, 128, n, -1)
    if fmt == "e4m3":
        vals = words.view(ml_dtypes.float8_e4m3fn).astype(np.float64)
    else:
        nib = np.empty((g, 128, n, 4), np.uint8)
        nib[..., 0::2] = words & 0xF
        nib[..., 1::2] = words >> 4
        vals = E2M1[nib]
    vals = vals * np.repeat(np.exp2(scales.astype(np.float64) - 127.0), 8, axis=1)[..., None]
    return vals.transpose(0, 1, 3, 2).reshape(g * 512, n)


def gelu(v):
    return 0.5 * v * (1.0 + np.tanh(np.sqrt(2.0 / np.pi) * (v + 0.044715 * v**3)))


K, T, S, S2 = 1024, 2048, 1024, 512

def setup_inputs():
    n = np.random.standard_normal
    s = mx_kscale(K)[:, None]
    d = {}
    d["tab_words"], d["tab_scales"] = pack_weight(n((K, T)) * s, "e4m3")
    d["offs"] = striped(np.random.permutation(T)[:S])
    d["offs2"] = striped(np.random.permutation(T)[:S2])
    d["w1"] = (1.5 * n((K, K)) / K**0.5 / s).astype(np.float32)
    d["gain"] = (1.3 * np.exp(0.3 * n(K)) / K**0.5 / s[:, 0]).astype(np.float32)
    d["w4_words"], d["w4_scales"] = pack_weight(n((K, K)) / K**0.5 / s * s.T, "e2m1")
    d["seat"] = np.exp(0.4 * n(S2)).astype(np.float32)
    return d

def reference(tab_words, tab_scales, offs, offs2, w1, gain, w4_words, w4_scales, seat):
    TW = unpack_weight(tab_words, tab_scales, "e4m3")
    v = TW[:, unstriped(offs)]
    v2 = TW[:, unstriped(offs2)]
    w4 = unpack_weight(w4_words, w4_scales, "e2m1")
    lin = mxq(f64(w1), 0, "e4m3").T @ v
    h = np.tanh(lin) * f64(gain)[:, None]
    hq = mxq(h, 0, "e4m3")
    b = np.abs(w4.T @ v2)
    e1 = v2.T @ hq
    e2 = mxq(b, 0, "e4m3").T @ hq
    return np.minimum(e1, e2) * f64(seat)[:, None]

@@ -1,0 +1,284 @@
+from contextlib import ExitStack
+
+import concourse.mybir as mybir
+from concourse.masks import make_identity
+
+K, T, S, S2 = 1024, 2048, 1024, 512
+FLOPS = 2 * K * K * S + 2 * K * K * S2 + 4 * K * S * S2
+
+F32 = mybir.dt.float32
+BF16 = mybir.dt.bfloat16
+I32 = mybir.dt.int32
+U32 = mybir.dt.uint32
+U16 = mybir.dt.uint16
+U8 = mybir.dt.uint8
+FP8X4 = mybir.dt.float8_e4m3fn_x4
+FP4X4 = mybir.dt.float4_e2m1fn_x4
+ACT = mybir.ActivationFunctionType
+ALU = mybir.AluOpType
+
+P = 128
+KP = 512
+PASSES = K // KP
+BANK = 512
+Q = 256
+VECTOR_CASTS = ((0, 1, 0), (0, 1, 1), (1, 1, 0), (1, 1, 1))
+SCALAR_SEATS = 4
+
+
+def tile_list_opposite_blade_match_kernel(
+    tc, tab_words, tab_scales, offs, offs2, w1, gain, w4_words, w4_scales, seat, out
+):
+    nc = tc.nc
+    with ExitStack() as ctx:
+        keep = ctx.enter_context(tc.tile_pool(name="keep", bufs=1))
+        ring = ctx.enter_context(tc.tile_pool(name="ring", bufs=4))
+        psum = ctx.enter_context(tc.psum_pool(name="psum", bufs=8))
+
+        def held(shape, dtype, name):
+            return keep.tile(shape, dtype, name=name, align_bytes=64)
+
+        def bank():
+            return psum.tile([P, BANK], F32, name="bank")
+
+        list2 = keep.tile([P, S2 // 16], U16, name="list2")
+        list1 = keep.tile([P, S // 16], U16, name="list1")
+        nc.sync.dma_start(list2[:], offs2)
+        nc.sync.dma_start(list1[:], offs)
+
+        tab_s = keep.tile([P, T], U8, name="tab_s", tag="load_c", align_bytes=64)
+        w4_s = held([P, PASSES, K], U8, "w4_s")
+        nc.vector.memset(tab_s[:].bitcast(I32), 0)
+        for quad in range(4):
+            nc.scalar.dma_start(
+                tab_s[32 * quad : 32 * quad + 8, :].bitcast(I32),
+                tab_scales[:, 4 * quad : 4 * quad + 4, :].bitcast(I32),
+            )
+        nc.gpsimd.memset(w4_s[:].bitcast(I32), 0)
+        for quad in range(4):
+            nc.gpsimd.dma_start(
+                w4_s[32 * quad : 32 * quad + 4, :, :].bitcast(I32),
+                w4_scales[:, 4 * quad : 4 * quad + 4, :].rearrange("a q n -> q a n").bitcast(I32),
+            )
+        ident = held([P, P], F32, "ident")
+        make_identity(nc, ident[:])
+        gain_t = held([P, PASSES, 4], F32, "gain_t")
+        seat_t = held([P, S2 // P], F32, "seat_t")
+        nc.gpsimd.dma_start(gain_t[:], gain.rearrange("(b p t) -> p b t", b=PASSES, t=4))
+        with nc.allow_non_contiguous_dma(reason="one seat factor for each output row"):
+            nc.gpsimd.dma_start(seat_t[:], seat.rearrange("(i p) -> p i", p=P))
+
+        warm = held([P, 2], F32, "warm")
+        nc.vector.memset(warm[:, 0:1], 0.0)
+        nc.scalar.activation(warm[:, 1:2], warm[:, 0:1], ACT.Tanh)
+
+        tab_w = [keep.tile([P, T], U32, name=f"tab_w{a}", tag=("load_a", "load_d")[a], align_bytes=64) for a in range(PASSES)]
+        w4_w = held([P, PASSES, 2 * K], U8, "w4_w")
+        w1_raw = {}
+        w1_tag = {(0, 0): "load_b", (0, 1): "load_c", (1, 0): "load_b", (1, 1): "load_a"}
+
+        def load_tab(a):
+            nc.sync.dma_start(tab_w[a][:].bitcast(I32), tab_words[a].rearrange("p n t -> p (n t)").bitcast(I32))
+
+        def load_w1(b, a):
+            w1_raw[b, a] = keep.tile([P, 4, KP], F32, name=f"w1_raw{b}{a}", tag=w1_tag[b, a], align_bytes=64)
+            nc.sync.dma_start(
+                w1_raw[b, a][:],
+                w1[KP * a : KP * (a + 1), KP * b : KP * (b + 1)].rearrange("(p j) c -> p j c", j=4),
+            )
+
+        load_tab(0)
+        nc.sync.dma_start(w4_w[:].bitcast(I32), w4_words.rearrange("a p n -> p a n").bitcast(I32))
+        load_w1(0, 0)
+        load_tab(1)
+
+        v2_w = [held([P, S2], U32, f"v2_w{a}") for a in range(PASSES)]
+        v2_s = held([P, S2], U8, "v2_s")
+        v2_s1 = held([P, S2], U8, "v2_s1")
+        v_w = {(a, h): held([P, BANK], U32, f"v_w{a}{h}") for a in range(PASSES) for h in range(2)}
+        v_s = [held([P, BANK], U8, f"v_s{h}") for h in range(2)]
+
+        def half_list(h):
+            return list1[:, 32 * h : 32 * (h + 1)]
+
+        nc.vector.memset(v2_s1[:].bitcast(I32), 0)
+        nc.vector.tensor_copy(v2_s[:], tab_s[:].indirect(list2[:]))
+        nc.scalar.dma_start(v2_s1[0:124, :].bitcast(I32), v2_s[4:128, :].bitcast(I32))
+        v2_planes = [v2_s, v2_s1]
+        for h in range(2):
+            nc.vector.tensor_copy(v_s[h][:], tab_s[:].indirect(half_list(h)))
+        load_w1(0, 1)
+
+        def gather_words(a):
+            nc.vector.tensor_copy(v2_w[a][:], tab_w[a][:].indirect(list2[:]))
+            for h in range(2):
+                nc.vector.tensor_copy(v_w[a, h][:], tab_w[a][:].indirect(half_list(h)))
+
+        w1_c = {}
+        w1_s = {}
+        w1_g = {}
+
+        def cast_w1(b, a):
+            g = held([P, 4, P, 4], BF16, f"w1_g{b}{a}")
+            w1_g[b, a] = g
+            for hm in range(2):
+                ms = slice(64 * hm, 64 * (hm + 1))
+                src = w1_raw[b, a][:].rearrange("p j (m t) -> p m j t", t=4)[:, ms]
+                dst = g[:].rearrange("p t m j -> p m j t")[:, ms]
+                if (b, a, hm) in VECTOR_CASTS:
+                    nc.vector.tensor_copy(dst, src)
+                else:
+                    nc.scalar.copy(dst, src)
+
+        def quant_w1(b, a):
+            w1_c[b, a] = held([P, KP], U32, f"w1_c{b}{a}")
+            w1_s[b, a] = held([P, KP], U8, f"w1_s{b}{a}")
+            nc.vector.quantize_mx(
+                w1_c[b, a][:].bitcast(FP8X4), w1_s[b, a][:], w1_g[b, a][:].rearrange("p t m j -> p (t m j)")
+            )
+
+        b_banks = {}
+
+        def project(a):
+            for b in range(PASSES):
+                for i in range(4):
+                    if a == 0:
+                        b_banks[b, i] = bank()
+                    nc.tensor.matmul_mx(
+                        b_banks[b, i][:],
+                        lhsT=v2_w[a][:, P * i : P * (i + 1)].bitcast(FP8X4),
+                        lhsT_scale=v2_planes[a][:, P * i : P * (i + 1)],
+                        rhs=w4_w[:, a, 2 * KP * b : 2 * KP * (b + 1)].bitcast(FP4X4),
+                        rhs_scale=w4_s[:, a, KP * b : KP * (b + 1)],
+                        start=(a == 0),
+                        stop=(a == PASSES - 1),
+                    )
+
+        b_abs = {}
+
+        def abs_b(b):
+            for i in range(4):
+                b_abs[b, i] = held([P, 2, P, 2], BF16, f"b_abs{b}{i}")
+                nc.scalar.activation(
+                    b_abs[b, i][:], b_banks[b, i][:].rearrange("m (p u e) -> m u p e", u=2, e=2), ACT.Abs
+                )
+
+        b_c = {}
+        b_s = {}
+
+        def turn_b(b):
+            g = held([P, S2, 4], BF16, f"b_g{b}")
+            for pair in range(2):
+                turned = bank()
+                for ii in range(2):
+                    words = b_abs[b, 2 * pair + ii][:].rearrange("m u p e -> m (u p e)").bitcast(F32)
+                    for u in range(2):
+                        nc.tensor.transpose(
+                            turned[:, Q * u + P * ii : Q * u + P * (ii + 1)], words[:, P * u : P * (u + 1)], ident[:]
+                        )
+                nc.scalar.copy(
+                    g[:, Q * pair : Q * (pair + 1), :].rearrange("p m t -> p (m t)").bitcast(F32).rearrange("p (m u) -> p m u", u=2),
+                    turned[:].rearrange("p (u m) -> p m u", u=2),
+                )
+            b_c[b] = held([P, S2], U32, f"b_c{b}")
+            b_s[b] = held([P, S2], U8, f"b_s{b}")
+            nc.vector.quantize_mx(b_c[b][:].bitcast(FP8X4), b_s[b][:], g[:].rearrange("p m t -> p (m t)"))
+
+        h_c = {(b, h): held([P, BANK], U32, f"h_c{b}{h}") for b in range(PASSES) for h in range(2)}
+        h_s = {(b, h): held([P, BANK], U8, f"h_s{b}{h}") for b in range(PASSES) for h in range(2)}
+        h_g = {}
+
+        def state(b, q):
+            h, cols = q // 2, slice(Q * (q % 2), Q * (q % 2 + 1))
+            th = ring.tile([P, 2, Q, 2], F32, name="th")
+            for u in range(2):
+                lin = bank()
+                for e in range(2):
+                    t = 2 * u + e
+                    for a in range(PASSES):
+                        nc.tensor.matmul_mx(
+                            lin[:, Q * e : Q * (e + 1)],
+                            lhsT=w1_c[b, a][:, P * t : P * (t + 1)].bitcast(FP8X4),
+                            lhsT_scale=w1_s[b, a][:, P * t : P * (t + 1)],
+                            rhs=v_w[a, h][:, cols].bitcast(FP8X4),
+                            rhs_scale=v_s[h][4 * a : P, cols],
+                            start=(a == 0),
+                            stop=(a == PASSES - 1),
+                        )
+                nc.scalar.activation(th[:, u], lin[:].rearrange("p (e n) -> p n e", e=2), ACT.Tanh)
+            g = ring.tile([P, Q, 2, 2], BF16, name="h_g", align_bytes=64)
+            h_g[b, q] = g
+            nc.vector.tensor_tensor(
+                g[:],
+                th[:].rearrange("p u n e -> p n u e"),
+                gain_t[:, b : b + 1, :].rearrange("p o (u e) -> p o u e", u=2).to_broadcast([P, Q, 2, 2]),
+                ALU.mult,
+            )
+
+        def quant_h(b, q):
+            h, cols = q // 2, slice(Q * (q % 2), Q * (q % 2 + 1))
+            nc.vector.quantize_mx(
+                h_c[b, h][:, cols].bitcast(FP8X4), h_s[b, h][:, cols], h_g[b, q][:].rearrange("p n u e -> p (n u e)")
+            )
+
+        def match(h, i):
+            ms = slice(P * i, P * (i + 1))
+            e2 = bank()
+            e1 = bank()
+            for acc, codes, planes in ((e2, b_c, b_s), (e1, v2_w, v2_planes)):
+                for b in range(PASSES):
+                    nc.tensor.matmul_mx(
+                        acc[:],
+                        lhsT=codes[b][:, ms].bitcast(FP8X4),
+                        lhsT_scale=planes[b][:, ms],
+                        rhs=h_c[b, h][:].bitcast(FP8X4),
+                        rhs_scale=h_s[b, h][:],
+                        start=(b == 0),
+                        stop=(b == PASSES - 1),
+                    )
+            e2_sb = ring.tile([P, BANK], F32, name="e2_sb")
+            nc.scalar.copy(e2_sb[:], e2[:])
+            low = ring.tile([P, BANK], F32, name="low")
+            nc.vector.tensor_tensor(low[:], e1[:], e2_sb[:], ALU.min)
+            return low
+
+        def finish(h, i, low):
+            res = ring.tile([P, BANK], F32, name="res")
+            if 4 * h + i < SCALAR_SEATS:
+                nc.scalar.activation(res[:], low[:], ACT.Copy, scale=seat_t[:, i : i + 1])
+            else:
+                nc.vector.tensor_scalar_mul(res[:], low[:], seat_t[:, i : i + 1])
+            nc.sync.dma_start(out[P * i : P * (i + 1), BANK * h : BANK * (h + 1)], res[:])
+
+        gather_words(0)
+        project(0)
+        cast_w1(0, 0)
+        load_w1(1, 0)
+        load_w1(1, 1)
+        quant_w1(0, 0)
+        gather_words(1)
+        project(1)
+        abs_b(0)
+        cast_w1(0, 1)
+        quant_w1(0, 1)
+        abs_b(1)
+        turn_b(0)
+        turn_b(1)
+        cast_w1(1, 0)
+        state(0, 0)
+        cast_w1(1, 1)
+        quant_w1(1, 0)
+        quant_w1(1, 1)
+        units = [(b, q) for b in range(PASSES) for q in range(4)]
+        for n in range(1, len(units)):
+            state(*units[n])
+            quant_h(*units[n - 1])
+        quant_h(*units[-1])
+        tiles = [(h, i) for h in range(2) for i in range(4)]
+        last = None
+        for h, i in tiles:
+            low = match(h, i)
+            if last is not None:
+                finish(*last)
+            last = (h, i, low)
+        finish(*last)

@@ -22,8 +22,8 @@ KP = 512
 PASSES = K // KP
 BANK = 512
 Q = 256
-VECTOR_CASTS = ((0, 1, 0), (0, 1, 1), (1, 1, 0), (1, 1, 1))
-SCALAR_SEATS = 4
+VECTOR_CASTS = ((1, 0, 0), (1, 0, 1), (1, 1, 0), (1, 1, 1))
+SCALAR_SEATS = 6
 
 
 def tile_list_opposite_blade_match_kernel(
@@ -46,15 +46,19 @@ def tile_list_opposite_blade_match_kernel(
         nc.sync.dma_start(list2[:], offs2)
         nc.sync.dma_start(list1[:], offs)
 
-        tab_s = keep.tile([P, T], U8, name="tab_s", tag="load_c", align_bytes=64)
+        tab_s = keep.tile([P, T], U8, name="tab_s", tag="load_d", align_bytes=64)
         w4_s = held([P, PASSES, K], U8, "w4_s")
+        warm_in = keep.tile([P, 1], F32, name="warm_in", tag="load_b", align_bytes=64)
+        warm_out = keep.tile([P, 1], F32, name="warm_out", tag="load_c", align_bytes=64)
         nc.vector.memset(tab_s[:].bitcast(I32), 0)
+        nc.vector.memset(warm_in[:], 0.0)
+        nc.gpsimd.memset(w4_s[:].bitcast(I32), 0)
         for quad in range(4):
             nc.scalar.dma_start(
                 tab_s[32 * quad : 32 * quad + 8, :].bitcast(I32),
                 tab_scales[:, 4 * quad : 4 * quad + 4, :].bitcast(I32),
             )
-        nc.gpsimd.memset(w4_s[:].bitcast(I32), 0)
+        nc.scalar.activation(warm_out[:], warm_in[:], ACT.Tanh)
         for quad in range(4):
             nc.gpsimd.dma_start(
                 w4_s[32 * quad : 32 * quad + 4, :, :].bitcast(I32),
@@ -62,22 +66,13 @@ def tile_list_opposite_blade_match_kernel(
             )
         ident = held([P, P], F32, "ident")
         make_identity(nc, ident[:])
-        gain_t = held([P, PASSES, 4], F32, "gain_t")
-        seat_t = held([P, S2 // P], F32, "seat_t")
-        nc.gpsimd.dma_start(gain_t[:], gain.rearrange("(b p t) -> p b t", b=PASSES, t=4))
-        with nc.allow_non_contiguous_dma(reason="one seat factor for each output row"):
-            nc.gpsimd.dma_start(seat_t[:], seat.rearrange("(i p) -> p i", p=P))
 
-        warm = held([P, 2], F32, "warm")
-        nc.vector.memset(warm[:, 0:1], 0.0)
-        nc.scalar.activation(warm[:, 1:2], warm[:, 0:1], ACT.Tanh)
-
-        tab_w = [keep.tile([P, T], U32, name=f"tab_w{a}", tag=("load_a", "load_d")[a], align_bytes=64) for a in range(PASSES)]
-        w4_w = held([P, PASSES, 2 * K], U8, "w4_w")
+        tab_w = {}
         w1_raw = {}
         w1_tag = {(0, 0): "load_b", (0, 1): "load_c", (1, 0): "load_b", (1, 1): "load_a"}
 
         def load_tab(a):
+            tab_w[a] = keep.tile([P, T], U32, name=f"tab_w{a}", tag=("load_a", "load_d")[a], align_bytes=64)
             nc.sync.dma_start(tab_w[a][:].bitcast(I32), tab_words[a].rearrange("p n t -> p (n t)").bitcast(I32))
 
         def load_w1(b, a):
@@ -88,38 +83,45 @@ def tile_list_opposite_blade_match_kernel(
             )
 
         load_tab(0)
+        w4_w = held([P, PASSES, 2 * K], U8, "w4_w")
         nc.sync.dma_start(w4_w[:].bitcast(I32), w4_words.rearrange("a p n -> p a n").bitcast(I32))
         load_w1(0, 0)
-        load_tab(1)
+        load_w1(0, 1)
 
         v2_w = [held([P, S2], U32, f"v2_w{a}") for a in range(PASSES)]
         v2_s = held([P, S2], U8, "v2_s")
         v2_s1 = held([P, S2], U8, "v2_s1")
-        v_w = {(a, h): held([P, BANK], U32, f"v_w{a}{h}") for a in range(PASSES) for h in range(2)}
-        v_s = [held([P, BANK], U8, f"v_s{h}") for h in range(2)]
+        v_w0 = held([P, S], U32, "v_w0")
+        v_w1 = [held([P, BANK], U32, f"v_w1{h}") for h in range(2)]
+        v_w = {(0, h): v_w0[:, BANK * h : BANK * (h + 1)] for h in range(2)}
+        for h in range(2):
+            v_w[1, h] = v_w1[h][:]
+        v_s_all = held([P, S], U8, "v_s")
+        v_s = [v_s_all[:, BANK * h : BANK * (h + 1)] for h in range(2)]
 
         def half_list(h):
             return list1[:, 32 * h : 32 * (h + 1)]
 
         nc.vector.memset(v2_s1[:].bitcast(I32), 0)
         nc.vector.tensor_copy(v2_s[:], tab_s[:].indirect(list2[:]))
-        nc.scalar.dma_start(v2_s1[0:124, :].bitcast(I32), v2_s[4:128, :].bitcast(I32))
+        nc.sync.dma_start(v2_s1[0:124, :].bitcast(I32), v2_s[4:128, :].bitcast(I32))
         v2_planes = [v2_s, v2_s1]
-        for h in range(2):
-            nc.vector.tensor_copy(v_s[h][:], tab_s[:].indirect(half_list(h)))
-        load_w1(0, 1)
+        nc.vector.tensor_copy(v_s_all[:], tab_s[:].indirect(list1[:]))
+        load_tab(1)
+        nc.vector.tensor_copy(v2_w[0][:], tab_w[0][:].indirect(list2[:]))
+        nc.vector.tensor_copy(v_w0[:], tab_w[0][:].indirect(list1[:]))
 
-        def gather_words(a):
-            nc.vector.tensor_copy(v2_w[a][:], tab_w[a][:].indirect(list2[:]))
+        def gather_second():
+            nc.vector.tensor_copy(v2_w[1][:], tab_w[1][:].indirect(list2[:]))
             for h in range(2):
-                nc.vector.tensor_copy(v_w[a, h][:], tab_w[a][:].indirect(half_list(h)))
+                nc.vector.tensor_copy(v_w1[h][:], tab_w[1][:].indirect(half_list(h)))
 
         w1_c = {}
         w1_s = {}
         w1_g = {}
 
         def cast_w1(b, a):
-            g = held([P, 4, P, 4], BF16, f"w1_g{b}{a}")
+            g = keep.tile([P, 4, P, 4], BF16, name=f"w1_g{b}{a}", tag=f"w1_g{a}", align_bytes=64)
             w1_g[b, a] = g
             for hm in range(2):
                 ms = slice(64 * hm, 64 * (hm + 1))
@@ -188,97 +190,106 @@ def tile_list_opposite_blade_match_kernel(
         h_s = {(b, h): held([P, BANK], U8, f"h_s{b}{h}") for b in range(PASSES) for h in range(2)}
         h_g = {}
 
-        def state(b, q):
-            h, cols = q // 2, slice(Q * (q % 2), Q * (q % 2 + 1))
-            th = ring.tile([P, 2, Q, 2], F32, name="th")
-            for u in range(2):
-                lin = bank()
-                for e in range(2):
-                    t = 2 * u + e
-                    for a in range(PASSES):
-                        nc.tensor.matmul_mx(
-                            lin[:, Q * e : Q * (e + 1)],
-                            lhsT=w1_c[b, a][:, P * t : P * (t + 1)].bitcast(FP8X4),
-                            lhsT_scale=w1_s[b, a][:, P * t : P * (t + 1)],
-                            rhs=v_w[a, h][:, cols].bitcast(FP8X4),
-                            rhs_scale=v_s[h][4 * a : P, cols],
-                            start=(a == 0),
-                            stop=(a == PASSES - 1),
-                        )
-                nc.scalar.activation(th[:, u], lin[:].rearrange("p (e n) -> p n e", e=2), ACT.Tanh)
-            g = ring.tile([P, Q, 2, 2], BF16, name="h_g", align_bytes=64)
-            h_g[b, q] = g
+        def state(b, h):
+            th = ring.tile([P, 2, BANK, 2], F32, name="th", bufs=3)
+            for q in range(2):
+                cols = slice(Q * q, Q * (q + 1))
+                for u in range(2):
+                    lin = bank()
+                    for e in range(2):
+                        t = 2 * u + e
+                        for a in range(PASSES):
+                            nc.tensor.matmul_mx(
+                                lin[:, Q * e : Q * (e + 1)],
+                                lhsT=w1_c[b, a][:, P * t : P * (t + 1)].bitcast(FP8X4),
+                                lhsT_scale=w1_s[b, a][:, P * t : P * (t + 1)],
+                                rhs=v_w[a, h][:, cols].bitcast(FP8X4),
+                                rhs_scale=v_s[h][4 * a : P, cols],
+                                start=(a == 0),
+                                stop=(a == PASSES - 1),
+                            )
+                    nc.scalar.activation(th[:, u, cols, :], lin[:].rearrange("p (e n) -> p n e", e=2), ACT.Tanh)
+            g = ring.tile([P, BANK, 2, 2], BF16, name="h_g", align_bytes=64)
+            h_g[b, h] = g
             nc.vector.tensor_tensor(
                 g[:],
                 th[:].rearrange("p u n e -> p n u e"),
-                gain_t[:, b : b + 1, :].rearrange("p o (u e) -> p o u e", u=2).to_broadcast([P, Q, 2, 2]),
+                gain_t[:, b : b + 1, :].rearrange("p o (u e) -> p o u e", u=2).to_broadcast([P, BANK, 2, 2]),
                 ALU.mult,
             )
 
-        def quant_h(b, q):
-            h, cols = q // 2, slice(Q * (q % 2), Q * (q % 2 + 1))
+        def quant_h(b, h):
             nc.vector.quantize_mx(
-                h_c[b, h][:, cols].bitcast(FP8X4), h_s[b, h][:, cols], h_g[b, q][:].rearrange("p n u e -> p (n u e)")
+                h_c[b, h][:].bitcast(FP8X4), h_s[b, h][:], h_g[b, h][:].rearrange("p n u e -> p (n u e)")
             )
 
-        def match(h, i):
+        def match(h, i, lo, hi):
             ms = slice(P * i, P * (i + 1))
             e2 = bank()
             e1 = bank()
+            width = hi - lo
             for acc, codes, planes in ((e2, b_c, b_s), (e1, v2_w, v2_planes)):
                 for b in range(PASSES):
                     nc.tensor.matmul_mx(
-                        acc[:],
+                        acc[:, :width],
                         lhsT=codes[b][:, ms].bitcast(FP8X4),
                         lhsT_scale=planes[b][:, ms],
-                        rhs=h_c[b, h][:].bitcast(FP8X4),
-                        rhs_scale=h_s[b, h][:],
+                        rhs=h_c[b, h][:, lo:hi].bitcast(FP8X4),
+                        rhs_scale=h_s[b, h][:, lo:hi],
                         start=(b == 0),
                         stop=(b == PASSES - 1),
                     )
             e2_sb = ring.tile([P, BANK], F32, name="e2_sb")
-            nc.scalar.copy(e2_sb[:], e2[:])
+            nc.scalar.copy(e2_sb[:, :width], e2[:, :width])
             low = ring.tile([P, BANK], F32, name="low")
-            nc.vector.tensor_tensor(low[:], e1[:], e2_sb[:], ALU.min)
+            nc.vector.tensor_tensor(low[:, :width], e1[:, :width], e2_sb[:, :width], ALU.min)
             return low
 
-        def finish(h, i, low):
+        def finish(h, i, lo, hi, low):
             res = ring.tile([P, BANK], F32, name="res")
+            width = hi - lo
             if 4 * h + i < SCALAR_SEATS:
-                nc.scalar.activation(res[:], low[:], ACT.Copy, scale=seat_t[:, i : i + 1])
+                nc.scalar.activation(res[:, :width], low[:, :width], ACT.Copy, scale=seat_t[:, i : i + 1])
             else:
-                nc.vector.tensor_scalar_mul(res[:], low[:], seat_t[:, i : i + 1])
-            nc.sync.dma_start(out[P * i : P * (i + 1), BANK * h : BANK * (h + 1)], res[:])
+                nc.vector.tensor_scalar_mul(res[:, :width], low[:, :width], seat_t[:, i : i + 1])
+            nc.sync.dma_start(out[P * i : P * (i + 1), BANK * h + lo : BANK * h + hi], res[:, :width])
 
-        gather_words(0)
         project(0)
         cast_w1(0, 0)
-        load_w1(1, 0)
         load_w1(1, 1)
+        load_w1(1, 0)
         quant_w1(0, 0)
-        gather_words(1)
+        cast_w1(0, 1)
+        gain_t = keep.tile([P, PASSES, 4], F32, name="gain_t", tag="load_c", align_bytes=64)
+        nc.sync.dma_start(gain_t[:], gain.rearrange("(b p t) -> p b t", b=PASSES, t=4))
+        gather_second()
+        seat_t = keep.tile([P, S2 // P], F32, name="seat_t", tag="load_d", align_bytes=64)
+        with nc.allow_non_contiguous_dma(reason="one seat factor for each output row"):
+            nc.sync.dma_start(seat_t[:], seat.rearrange("(i p) -> p i", p=P))
+        quant_w1(0, 1)
         project(1)
         abs_b(0)
-        cast_w1(0, 1)
-        quant_w1(0, 1)
-        abs_b(1)
-        turn_b(0)
-        turn_b(1)
-        cast_w1(1, 0)
         state(0, 0)
         cast_w1(1, 1)
-        quant_w1(1, 0)
+        cast_w1(1, 0)
         quant_w1(1, 1)
-        units = [(b, q) for b in range(PASSES) for q in range(4)]
-        for n in range(1, len(units)):
-            state(*units[n])
-            quant_h(*units[n - 1])
-        quant_h(*units[-1])
-        tiles = [(h, i) for h in range(2) for i in range(4)]
+        quant_w1(1, 0)
+        abs_b(1)
+        turn_b(0)
+        state(1, 0)
+        quant_h(0, 0)
+        turn_b(1)
+        quant_h(1, 0)
+        state(0, 1)
+        state(1, 1)
+        quant_h(0, 1)
+        quant_h(1, 1)
+        tiles = [(h, i, 0, BANK) for h in range(2) for i in range(4)]
+        tiles = tiles[:-1] + [(1, 3, 0, Q), (1, 3, Q, BANK)]
         last = None
-        for h, i in tiles:
-            low = match(h, i)
+        for piece in tiles:
+            low = match(*piece)
             if last is not None:
                 finish(*last)
-            last = (h, i, low)
+            last = piece + (low,)
         finish(*last)

@@ -22,8 +22,6 @@ KP = 512
 PASSES = K // KP
 BANK = 512
 Q = 256
-VECTOR_CASTS = ((1, 0, 0), (1, 0, 1), (1, 1, 0), (1, 1, 1))
-SCALAR_SEATS = 6
 
 
 def tile_list_opposite_blade_match_kernel(
@@ -32,105 +30,106 @@ def tile_list_opposite_blade_match_kernel(
     nc = tc.nc
     with ExitStack() as ctx:
         keep = ctx.enter_context(tc.tile_pool(name="keep", bufs=1))
-        ring = ctx.enter_context(tc.tile_pool(name="ring", bufs=4))
-        psum = ctx.enter_context(tc.psum_pool(name="psum", bufs=8))
+        ring = ctx.enter_context(tc.tile_pool(name="ring", bufs=9))
+        psum = ctx.enter_context(tc.psum_pool(name="psum", bufs=1))
 
-        def held(shape, dtype, name):
-            return keep.tile(shape, dtype, name=name, align_bytes=64)
+        def held(shape, dtype, name, slot=None):
+            return keep.tile(shape, dtype, name=name, tag=slot or name, align_bytes=64)
 
-        def bank():
-            return psum.tile([P, BANK], F32, name="bank")
+        def bank(n):
+            return psum.tile([P, BANK], F32, name=f"bank{n % 8}")
 
         list2 = keep.tile([P, S2 // 16], U16, name="list2")
         list1 = keep.tile([P, S // 16], U16, name="list1")
         nc.sync.dma_start(list2[:], offs2)
         nc.sync.dma_start(list1[:], offs)
 
-        tab_s = keep.tile([P, T], U8, name="tab_s", tag="load_d", align_bytes=64)
+        tab_s = held([P, T], U8, "tab_s", "slot_s")
         w4_s = held([P, PASSES, K], U8, "w4_s")
-        warm_in = keep.tile([P, 1], F32, name="warm_in", tag="load_b", align_bytes=64)
-        warm_out = keep.tile([P, 1], F32, name="warm_out", tag="load_c", align_bytes=64)
+        warm_in = held([P, 1], F32, "warm_in", "slot_b")
+        warm_out = held([P, 1], F32, "warm_out", "slot_c")
+        warm_bias = held([P, 1], F32, "warm_bias", "slot_d")
         nc.vector.memset(tab_s[:].bitcast(I32), 0)
         nc.vector.memset(warm_in[:], 0.0)
-        nc.gpsimd.memset(w4_s[:].bitcast(I32), 0)
+        nc.vector.memset(warm_bias[:], 0.0)
         for quad in range(4):
             nc.scalar.dma_start(
                 tab_s[32 * quad : 32 * quad + 8, :].bitcast(I32),
                 tab_scales[:, 4 * quad : 4 * quad + 4, :].bitcast(I32),
             )
-        nc.scalar.activation(warm_out[:], warm_in[:], ACT.Tanh)
-        for quad in range(4):
-            nc.gpsimd.dma_start(
+        nc.scalar.activation(warm_out[:], warm_in[:], ACT.Tanh, bias=warm_bias[:])
+        nc.gpsimd.memset(w4_s[:].bitcast(I32), 0)
+
+        def load_w4_scales(engine, quad):
+            engine.dma_start(
                 w4_s[32 * quad : 32 * quad + 4, :, :].bitcast(I32),
                 w4_scales[:, 4 * quad : 4 * quad + 4, :].rearrange("a q n -> q a n").bitcast(I32),
             )
+
+        for quad in range(3):
+            load_w4_scales(nc.gpsimd, quad)
         ident = held([P, P], F32, "ident")
         make_identity(nc, ident[:])
 
         tab_w = {}
         w1_raw = {}
-        w1_tag = {(0, 0): "load_b", (0, 1): "load_c", (1, 0): "load_b", (1, 1): "load_a"}
 
-        def load_tab(a):
-            tab_w[a] = keep.tile([P, T], U32, name=f"tab_w{a}", tag=("load_a", "load_d")[a], align_bytes=64)
+        def load_tab(a, slot):
+            tab_w[a] = held([P, T], U32, f"tab_w{a}", slot)
             nc.sync.dma_start(tab_w[a][:].bitcast(I32), tab_words[a].rearrange("p n t -> p (n t)").bitcast(I32))
 
-        def load_w1(b, a):
-            w1_raw[b, a] = keep.tile([P, 4, KP], F32, name=f"w1_raw{b}{a}", tag=w1_tag[b, a], align_bytes=64)
+        def load_w1(b, a, slot):
+            w1_raw[b, a] = held([P, 4, KP], F32, f"w1_raw{b}{a}", slot)
             nc.sync.dma_start(
                 w1_raw[b, a][:],
                 w1[KP * a : KP * (a + 1), KP * b : KP * (b + 1)].rearrange("(p j) c -> p j c", j=4),
             )
 
-        load_tab(0)
+        load_tab(0, "slot_a")
         w4_w = held([P, PASSES, 2 * K], U8, "w4_w")
         nc.sync.dma_start(w4_w[:].bitcast(I32), w4_words.rearrange("a p n -> p a n").bitcast(I32))
-        load_w1(0, 0)
-        load_w1(0, 1)
+        load_w4_scales(nc.sync, 3)
+        load_w1(0, 0, "slot_b")
+        load_w1(0, 1, "slot_c")
+        load_tab(1, "slot_d")
 
         v2_w = [held([P, S2], U32, f"v2_w{a}") for a in range(PASSES)]
-        v2_s = held([P, S2], U8, "v2_s")
         v2_s1 = held([P, S2], U8, "v2_s1")
         v_w0 = held([P, S], U32, "v_w0")
         v_w1 = [held([P, BANK], U32, f"v_w1{h}") for h in range(2)]
         v_w = {(0, h): v_w0[:, BANK * h : BANK * (h + 1)] for h in range(2)}
         for h in range(2):
             v_w[1, h] = v_w1[h][:]
-        v_s_all = held([P, S], U8, "v_s")
-        v_s = [v_s_all[:, BANK * h : BANK * (h + 1)] for h in range(2)]
-
-        def half_list(h):
-            return list1[:, 32 * h : 32 * (h + 1)]
 
         nc.vector.memset(v2_s1[:].bitcast(I32), 0)
-        nc.vector.tensor_copy(v2_s[:], tab_s[:].indirect(list2[:]))
-        nc.sync.dma_start(v2_s1[0:124, :].bitcast(I32), v2_s[4:128, :].bitcast(I32))
-        v2_planes = [v2_s, v2_s1]
-        nc.vector.tensor_copy(v_s_all[:], tab_s[:].indirect(list1[:]))
-        load_tab(1)
         nc.vector.tensor_copy(v2_w[0][:], tab_w[0][:].indirect(list2[:]))
         nc.vector.tensor_copy(v_w0[:], tab_w[0][:].indirect(list1[:]))
+        picked_s = held([P, S2 + S], U8, "picked_s", "slot_a")
+        v2_s = picked_s[:, :S2]
+        v_s = [picked_s[:, S2 + BANK * h : S2 + BANK * (h + 1)] for h in range(2)]
+        nc.vector.tensor_copy(v2_s, tab_s[:].indirect(list2[:]))
+        nc.sync.dma_start(v2_s1[0:124, :].bitcast(I32), v2_s[4:128, :].bitcast(I32))
+        v2_planes = [v2_s, v2_s1[:]]
+        nc.vector.tensor_copy(picked_s[:, S2:], tab_s[:].indirect(list1[:]))
 
         def gather_second():
             nc.vector.tensor_copy(v2_w[1][:], tab_w[1][:].indirect(list2[:]))
             for h in range(2):
-                nc.vector.tensor_copy(v_w1[h][:], tab_w[1][:].indirect(half_list(h)))
+                nc.vector.tensor_copy(v_w1[h][:], tab_w[1][:].indirect(list1[:, 32 * h : 32 * (h + 1)]))
 
         w1_c = {}
         w1_s = {}
         w1_g = {}
 
-        def cast_w1(b, a):
-            g = keep.tile([P, 4, P, 4], BF16, name=f"w1_g{b}{a}", tag=f"w1_g{a}", align_bytes=64)
+        def cast_w1(b, a, slot):
+            g = held([P, 4, P, 4], BF16, f"w1_g{b}{a}", slot)
             w1_g[b, a] = g
-            for hm in range(2):
-                ms = slice(64 * hm, 64 * (hm + 1))
-                src = w1_raw[b, a][:].rearrange("p j (m t) -> p m j t", t=4)[:, ms]
-                dst = g[:].rearrange("p t m j -> p m j t")[:, ms]
-                if (b, a, hm) in VECTOR_CASTS:
-                    nc.vector.tensor_copy(dst, src)
-                else:
-                    nc.scalar.copy(dst, src)
+            src = w1_raw[b, a][:].rearrange("p j (m t) -> p m j t", t=4)
+            dst = g[:].rearrange("p t m j -> p m j t")
+            if b == 1:
+                nc.vector.tensor_copy(dst, src)
+            else:
+                nc.scalar.copy(dst, src)
 
         def quant_w1(b, a):
             w1_c[b, a] = held([P, KP], U32, f"w1_c{b}{a}")
@@ -145,7 +144,7 @@ def tile_list_opposite_blade_match_kernel(
             for b in range(PASSES):
                 for i in range(4):
                     if a == 0:
-                        b_banks[b, i] = bank()
+                        b_banks[b, i] = bank(4 * b + i)
                     nc.tensor.matmul_mx(
                         b_banks[b, i][:],
                         lhsT=v2_w[a][:, P * i : P * (i + 1)].bitcast(FP8X4),
@@ -158,44 +157,50 @@ def tile_list_opposite_blade_match_kernel(
 
         b_abs = {}
 
-        def abs_b(b):
+        def abs_b(b, slot):
+            b_abs[b] = held([P, 4, 2, P, 2], BF16, f"b_abs{b}", slot)
             for i in range(4):
-                b_abs[b, i] = held([P, 2, P, 2], BF16, f"b_abs{b}{i}")
                 nc.scalar.activation(
-                    b_abs[b, i][:], b_banks[b, i][:].rearrange("m (p u e) -> m u p e", u=2, e=2), ACT.Abs
+                    b_abs[b][:, i], b_banks[b, i][:].rearrange("m (p u e) -> m u p e", u=2, e=2), ACT.Abs
                 )
 
         b_c = {}
         b_s = {}
+        b_g = {}
 
-        def turn_b(b):
+        def turn_b(b, first):
             g = held([P, S2, 4], BF16, f"b_g{b}")
+            b_g[b] = g
             for pair in range(2):
-                turned = bank()
+                turned = bank(first + pair)
                 for ii in range(2):
-                    words = b_abs[b, 2 * pair + ii][:].rearrange("m u p e -> m (u p e)").bitcast(F32)
+                    words = b_abs[b][:, 2 * pair + ii].rearrange("m u p e -> m (u p e)").bitcast(F32)
                     for u in range(2):
                         nc.tensor.transpose(
                             turned[:, Q * u + P * ii : Q * u + P * (ii + 1)], words[:, P * u : P * (u + 1)], ident[:]
                         )
-                nc.scalar.copy(
+                (nc.vector.tensor_copy if (b, pair) == (1, 0) else nc.scalar.copy)(
                     g[:, Q * pair : Q * (pair + 1), :].rearrange("p m t -> p (m t)").bitcast(F32).rearrange("p (m u) -> p m u", u=2),
                     turned[:].rearrange("p (u m) -> p m u", u=2),
                 )
+
+        def quant_b(b):
             b_c[b] = held([P, S2], U32, f"b_c{b}")
             b_s[b] = held([P, S2], U8, f"b_s{b}")
-            nc.vector.quantize_mx(b_c[b][:].bitcast(FP8X4), b_s[b][:], g[:].rearrange("p m t -> p (m t)"))
+            nc.vector.quantize_mx(b_c[b][:].bitcast(FP8X4), b_s[b][:], b_g[b][:].rearrange("p m t -> p (m t)"))
 
         h_c = {(b, h): held([P, BANK], U32, f"h_c{b}{h}") for b in range(PASSES) for h in range(2)}
         h_s = {(b, h): held([P, BANK], U8, f"h_s{b}{h}") for b in range(PASSES) for h in range(2)}
+        th = {}
         h_g = {}
 
-        def state(b, h):
-            th = ring.tile([P, 2, BANK, 2], F32, name="th", bufs=3)
+        def state(b, h, first):
+            th[b, h] = held([P, 2, BANK, 2], F32, f"th{b}{h}")
+            h_g[b, h] = held([P, BANK, 2, 2], BF16, f"h_g{b}{h}")
             for q in range(2):
                 cols = slice(Q * q, Q * (q + 1))
                 for u in range(2):
-                    lin = bank()
+                    lin = bank(first + 2 * q + u)
                     for e in range(2):
                         t = 2 * u + e
                         for a in range(PASSES):
@@ -208,25 +213,29 @@ def tile_list_opposite_blade_match_kernel(
                                 start=(a == 0),
                                 stop=(a == PASSES - 1),
                             )
-                    nc.scalar.activation(th[:, u, cols, :], lin[:].rearrange("p (e n) -> p n e", e=2), ACT.Tanh)
-            g = ring.tile([P, BANK, 2, 2], BF16, name="h_g", align_bytes=64)
-            h_g[b, h] = g
+                    nc.scalar.activation(th[b, h][:, u, cols, :], lin[:].rearrange("p (e n) -> p n e", e=2), ACT.Tanh)
+
+        def gain_h(b, h, lo=0, hi=BANK):
             nc.vector.tensor_tensor(
-                g[:],
-                th[:].rearrange("p u n e -> p n u e"),
-                gain_t[:, b : b + 1, :].rearrange("p o (u e) -> p o u e", u=2).to_broadcast([P, BANK, 2, 2]),
+                h_g[b, h][:, lo:hi],
+                th[b, h][:, :, lo:hi, :].rearrange("p u n e -> p n u e"),
+                gain_t[:, b : b + 1, :].rearrange("p o (u e) -> p o u e", u=2).to_broadcast([P, hi - lo, 2, 2]),
                 ALU.mult,
             )
 
-        def quant_h(b, h):
+        def quant_h(b, h, lo=0, hi=BANK):
             nc.vector.quantize_mx(
-                h_c[b, h][:].bitcast(FP8X4), h_s[b, h][:], h_g[b, h][:].rearrange("p n u e -> p (n u e)")
+                h_c[b, h][:, lo:hi].bitcast(FP8X4),
+                h_s[b, h][:, lo:hi],
+                h_g[b, h][:, lo:hi].rearrange("p n u e -> p (n u e)"),
             )
 
-        def match(h, i, lo, hi):
+        lows = {}
+
+        def match(h, i, lo, hi, first):
             ms = slice(P * i, P * (i + 1))
-            e2 = bank()
-            e1 = bank()
+            e2 = bank(first)
+            e1 = bank(first + 1)
             width = hi - lo
             for acc, codes, planes in ((e2, b_c, b_s), (e1, v2_w, v2_planes)):
                 for b in range(PASSES):
@@ -243,53 +252,61 @@ def tile_list_opposite_blade_match_kernel(
             nc.scalar.copy(e2_sb[:, :width], e2[:, :width])
             low = ring.tile([P, BANK], F32, name="low")
             nc.vector.tensor_tensor(low[:, :width], e1[:, :width], e2_sb[:, :width], ALU.min)
-            return low
+            lows[h, i, lo] = low
 
-        def finish(h, i, lo, hi, low):
+        def finish(h, i, lo, hi):
+            low = lows[h, i, lo]
             res = ring.tile([P, BANK], F32, name="res")
             width = hi - lo
-            if 4 * h + i < SCALAR_SEATS:
+            if 4 * h + i < 2:
                 nc.scalar.activation(res[:, :width], low[:, :width], ACT.Copy, scale=seat_t[:, i : i + 1])
+            elif 4 * h + i < 6:
+                nc.gpsimd.tensor_scalar(res[:, :width], low[:, :width], seat_t[:, i : i + 1], 0.0, ALU.mult, ALU.add)
             else:
                 nc.vector.tensor_scalar_mul(res[:, :width], low[:, :width], seat_t[:, i : i + 1])
             nc.sync.dma_start(out[P * i : P * (i + 1), BANK * h + lo : BANK * h + hi], res[:, :width])
 
         project(0)
-        cast_w1(0, 0)
-        load_w1(1, 1)
-        load_w1(1, 0)
+        cast_w1(0, 0, "stage_a")
+        load_w1(1, 0, "slot_b")
+        load_w1(1, 1, "slot_s")
         quant_w1(0, 0)
-        cast_w1(0, 1)
-        gain_t = keep.tile([P, PASSES, 4], F32, name="gain_t", tag="load_c", align_bytes=64)
+        cast_w1(0, 1, "stage_b")
+        gain_t = held([P, PASSES, 4], F32, "gain_t", "slot_c")
         nc.sync.dma_start(gain_t[:], gain.rearrange("(b p t) -> p b t", b=PASSES, t=4))
+        quant_w1(0, 1)
         gather_second()
-        seat_t = keep.tile([P, S2 // P], F32, name="seat_t", tag="load_d", align_bytes=64)
+        seat_t = held([P, S2 // P], F32, "seat_t", "slot_d")
         with nc.allow_non_contiguous_dma(reason="one seat factor for each output row"):
             nc.sync.dma_start(seat_t[:], seat.rearrange("(i p) -> p i", p=P))
-        quant_w1(0, 1)
         project(1)
-        abs_b(0)
-        state(0, 0)
-        cast_w1(1, 1)
-        cast_w1(1, 0)
-        quant_w1(1, 1)
+        abs_b(0, None)
+        state(0, 0, 0)
+        cast_w1(1, 0, "stage_b")
+        cast_w1(1, 1, "stage_a")
         quant_w1(1, 0)
-        abs_b(1)
-        turn_b(0)
-        state(1, 0)
+        quant_w1(1, 1)
+        gain_h(0, 0)
+        state(1, 0, 0)
+        abs_b(1, "slot_b")
         quant_h(0, 0)
-        turn_b(1)
+        turn_b(0, 4)
+        gain_h(1, 0)
+        turn_b(1, 6)
+        state(0, 1, 0)
+        quant_b(0)
         quant_h(1, 0)
-        state(0, 1)
-        state(1, 1)
+        quant_b(1)
+        gain_h(0, 1)
+        state(1, 1, 0)
+        match(0, 0, 0, BANK, 4)
         quant_h(0, 1)
+        gain_h(1, 1)
+        finish(0, 0, 0, BANK)
         quant_h(1, 1)
-        tiles = [(h, i, 0, BANK) for h in range(2) for i in range(4)]
-        tiles = tiles[:-1] + [(1, 3, 0, Q), (1, 3, Q, BANK)]
-        last = None
-        for piece in tiles:
-            low = match(*piece)
-            if last is not None:
-                finish(*last)
-            last = piece + (low,)
-        finish(*last)
+        pieces = [(h, i, 0, BANK) for h in range(2) for i in range(4)][:-1] + [(1, 3, 0, Q), (1, 3, Q, BANK)]
+        for n in range(1, len(pieces)):
+            match(*pieces[n], 4 + 2 * n)
+            if n > 1:
+                finish(*pieces[n - 1])
+        finish(*pieces[-1])

@@ -18,10 +18,13 @@ ACT = mybir.ActivationFunctionType
 ALU = mybir.AluOpType
 
 P = 128
-KP = 512
-PASSES = K // KP
+K_PASS = 512
+PASSES = K // K_PASS
 BANK = 512
-Q = 256
+QUARTER = 256
+PSUM_BANKS = 8
+OUT_PIECES = 9
+SCALAR_SEAT_TILES = 6
 
 
 def tile_list_opposite_blade_match_kernel(
@@ -30,221 +33,211 @@ def tile_list_opposite_blade_match_kernel(
     nc = tc.nc
     with ExitStack() as ctx:
         keep = ctx.enter_context(tc.tile_pool(name="keep", bufs=1))
-        ring = ctx.enter_context(tc.tile_pool(name="ring", bufs=9))
+        table = ctx.enter_context(tc.tile_pool(name="table", bufs=1))
+        ring = ctx.enter_context(tc.tile_pool(name="ring", bufs=OUT_PIECES))
         psum = ctx.enter_context(tc.psum_pool(name="psum", bufs=1))
 
-        def held(shape, dtype, name, slot=None):
-            return keep.tile(shape, dtype, name=name, tag=slot or name, align_bytes=64)
+        def held(shape, dtype, name, buffer=None):
+            return keep.tile(shape, dtype, name=name, tag=buffer or name, align_bytes=64)
+
+        def placed(shape, dtype, name, first_byte):
+            return table.tile(shape, dtype, name=name, align_bytes=64, offset=first_byte)
 
         def bank(n):
-            return psum.tile([P, BANK], F32, name=f"bank{n % 8}")
+            return psum.tile([P, BANK], F32, name=f"bank{n % PSUM_BANKS}")
 
         list2 = keep.tile([P, S2 // 16], U16, name="list2")
         list1 = keep.tile([P, S // 16], U16, name="list1")
         nc.sync.dma_start(list2[:], offs2)
         nc.sync.dma_start(list1[:], offs)
 
-        tab_s = held([P, T], U8, "tab_s", "slot_s")
+        tab_s = held([P, T], U8, "tab_s", "buf_tab_s")
         w4_s = held([P, PASSES, K], U8, "w4_s")
-        warm_in = held([P, 1], F32, "warm_in", "slot_b")
-        warm_out = held([P, 1], F32, "warm_out", "slot_c")
-        warm_bias = held([P, 1], F32, "warm_bias", "slot_d")
         nc.vector.memset(tab_s[:].bitcast(I32), 0)
-        nc.vector.memset(warm_in[:], 0.0)
-        nc.vector.memset(warm_bias[:], 0.0)
+        nc.gpsimd.memset(w4_s[:].bitcast(I32), 0)
         for quad in range(4):
             nc.scalar.dma_start(
                 tab_s[32 * quad : 32 * quad + 8, :].bitcast(I32),
                 tab_scales[:, 4 * quad : 4 * quad + 4, :].bitcast(I32),
             )
-        nc.scalar.activation(warm_out[:], warm_in[:], ACT.Tanh, bias=warm_bias[:])
-        nc.gpsimd.memset(w4_s[:].bitcast(I32), 0)
-
-        def load_w4_scales(engine, quad):
-            engine.dma_start(
+        for quad in range(4):
+            nc.gpsimd.dma_start(
                 w4_s[32 * quad : 32 * quad + 4, :, :].bitcast(I32),
                 w4_scales[:, 4 * quad : 4 * quad + 4, :].rearrange("a q n -> q a n").bitcast(I32),
             )
-
-        for quad in range(3):
-            load_w4_scales(nc.gpsimd, quad)
         ident = held([P, P], F32, "ident")
         make_identity(nc, ident[:])
 
         tab_w = {}
         w1_raw = {}
 
-        def load_tab(a, slot):
-            tab_w[a] = held([P, T], U32, f"tab_w{a}", slot)
+        def load_table(a, first_byte):
+            tab_w[a] = placed([P, T], U32, f"tab_w{a}", first_byte)
             nc.sync.dma_start(tab_w[a][:].bitcast(I32), tab_words[a].rearrange("p n t -> p (n t)").bitcast(I32))
 
-        def load_w1(b, a, slot):
-            w1_raw[b, a] = held([P, 4, KP], F32, f"w1_raw{b}{a}", slot)
+        def load_w1(b, a, buffer):
+            w1_raw[b, a] = held([P, 4, K_PASS], F32, f"w1_raw{b}{a}", buffer)
             nc.sync.dma_start(
                 w1_raw[b, a][:],
-                w1[KP * a : KP * (a + 1), KP * b : KP * (b + 1)].rearrange("(p j) c -> p j c", j=4),
+                w1[K_PASS * a : K_PASS * (a + 1), K_PASS * b : K_PASS * (b + 1)].rearrange("(p j) c -> p j c", j=4),
             )
 
-        load_tab(0, "slot_a")
+        load_table(0, 0)
         w4_w = held([P, PASSES, 2 * K], U8, "w4_w")
         nc.sync.dma_start(w4_w[:].bitcast(I32), w4_words.rearrange("a p n -> p a n").bitcast(I32))
-        load_w4_scales(nc.sync, 3)
-        load_w1(0, 0, "slot_b")
-        load_w1(0, 1, "slot_c")
-        load_tab(1, "slot_d")
+        load_w1(0, 0, "buf_w1_00")
+        load_w1(0, 1, "buf_w1_01")
 
         v2_w = [held([P, S2], U32, f"v2_w{a}") for a in range(PASSES)]
-        v2_s1 = held([P, S2], U8, "v2_s1")
         v_w0 = held([P, S], U32, "v_w0")
-        v_w1 = [held([P, BANK], U32, f"v_w1{h}") for h in range(2)]
-        v_w = {(0, h): v_w0[:, BANK * h : BANK * (h + 1)] for h in range(2)}
-        for h in range(2):
-            v_w[1, h] = v_w1[h][:]
+        v_w1 = [held([P, BANK], U32, f"v_w1{half}") for half in range(2)]
+        v_w = {(0, half): v_w0[:, BANK * half : BANK * (half + 1)] for half in range(2)}
+        for half in range(2):
+            v_w[1, half] = v_w1[half][:]
 
+        v2_s1 = held([P, S2], U8, "v2_s1")
         nc.vector.memset(v2_s1[:].bitcast(I32), 0)
         nc.vector.tensor_copy(v2_w[0][:], tab_w[0][:].indirect(list2[:]))
         nc.vector.tensor_copy(v_w0[:], tab_w[0][:].indirect(list1[:]))
-        picked_s = held([P, S2 + S], U8, "picked_s", "slot_a")
+        load_table(1, S2 + S)
+        picked_s = placed([P, S2 + S], U8, "picked_s", 0)
         v2_s = picked_s[:, :S2]
-        v_s = [picked_s[:, S2 + BANK * h : S2 + BANK * (h + 1)] for h in range(2)]
+        v_s = [picked_s[:, S2 + BANK * half : S2 + BANK * (half + 1)] for half in range(2)]
         nc.vector.tensor_copy(v2_s, tab_s[:].indirect(list2[:]))
-        nc.sync.dma_start(v2_s1[0:124, :].bitcast(I32), v2_s[4:128, :].bitcast(I32))
+        nc.sync.dma_start(v2_s1[0 : P - 4, :].bitcast(I32), v2_s[4:P, :].bitcast(I32))
         v2_planes = [v2_s, v2_s1[:]]
         nc.vector.tensor_copy(picked_s[:, S2:], tab_s[:].indirect(list1[:]))
 
-        def gather_second():
+        def gather_pass1():
             nc.vector.tensor_copy(v2_w[1][:], tab_w[1][:].indirect(list2[:]))
-            for h in range(2):
-                nc.vector.tensor_copy(v_w1[h][:], tab_w[1][:].indirect(list1[:, 32 * h : 32 * (h + 1)]))
+            for half in range(2):
+                entries = list1[:, BANK // 16 * half : BANK // 16 * (half + 1)]
+                nc.vector.tensor_copy(v_w1[half][:], tab_w[1][:].indirect(entries))
 
+        w1_bf = {}
         w1_c = {}
         w1_s = {}
-        w1_g = {}
 
-        def cast_w1(b, a, slot):
-            g = held([P, 4, P, 4], BF16, f"w1_g{b}{a}", slot)
-            w1_g[b, a] = g
-            src = w1_raw[b, a][:].rearrange("p j (m t) -> p m j t", t=4)
-            dst = g[:].rearrange("p t m j -> p m j t")
-            if b == 1:
-                nc.vector.tensor_copy(dst, src)
-            else:
-                nc.scalar.copy(dst, src)
+        def round_w1(b, a, copy, buffer):
+            w1_bf[b, a] = held([P, 4, P, 4], BF16, f"w1_bf{b}{a}", buffer)
+            copy(w1_bf[b, a][:].rearrange("p t n j -> p n t j"), w1_raw[b, a][:].rearrange("p j (n t) -> p n t j", t=4))
 
-        def quant_w1(b, a):
-            w1_c[b, a] = held([P, KP], U32, f"w1_c{b}{a}")
-            w1_s[b, a] = held([P, KP], U8, f"w1_s{b}{a}")
+        def quantise_w1(b, a):
+            w1_c[b, a] = held([P, K_PASS], U32, f"w1_c{b}{a}")
+            w1_s[b, a] = held([P, K_PASS], U8, f"w1_s{b}{a}")
             nc.vector.quantize_mx(
-                w1_c[b, a][:].bitcast(FP8X4), w1_s[b, a][:], w1_g[b, a][:].rearrange("p t m j -> p (t m j)")
+                w1_c[b, a][:].bitcast(FP8X4), w1_s[b, a][:], w1_bf[b, a][:].rearrange("p t n j -> p (t n j)")
             )
 
-        b_banks = {}
+        proj = {}
 
         def project(a):
             for b in range(PASSES):
                 for i in range(4):
                     if a == 0:
-                        b_banks[b, i] = bank(4 * b + i)
+                        proj[b, i] = bank(4 * b + i)
                     nc.tensor.matmul_mx(
-                        b_banks[b, i][:],
+                        proj[b, i][:],
                         lhsT=v2_w[a][:, P * i : P * (i + 1)].bitcast(FP8X4),
                         lhsT_scale=v2_planes[a][:, P * i : P * (i + 1)],
-                        rhs=w4_w[:, a, 2 * KP * b : 2 * KP * (b + 1)].bitcast(FP4X4),
-                        rhs_scale=w4_s[:, a, KP * b : KP * (b + 1)],
+                        rhs=w4_w[:, a, 2 * K_PASS * b : 2 * K_PASS * (b + 1)].bitcast(FP4X4),
+                        rhs_scale=w4_s[:, a, K_PASS * b : K_PASS * (b + 1)],
                         start=(a == 0),
                         stop=(a == PASSES - 1),
                     )
 
         b_abs = {}
 
-        def abs_b(b, slot):
-            b_abs[b] = held([P, 4, 2, P, 2], BF16, f"b_abs{b}", slot)
+        def abs_b(b, buffer):
+            b_abs[b] = held([P, 4, 2, P, 2], BF16, f"b_abs{b}", buffer)
             for i in range(4):
                 nc.scalar.activation(
-                    b_abs[b][:, i], b_banks[b, i][:].rearrange("m (p u e) -> m u p e", u=2, e=2), ACT.Abs
+                    b_abs[b][:, i], proj[b, i][:].rearrange("m (p u e) -> m u p e", u=2, e=2), ACT.Abs
                 )
 
+        b_bf = {}
         b_c = {}
         b_s = {}
-        b_g = {}
 
-        def turn_b(b, first):
-            g = held([P, S2, 4], BF16, f"b_g{b}")
-            b_g[b] = g
-            for pair in range(2):
-                turned = bank(first + pair)
-                for ii in range(2):
-                    words = b_abs[b][:, 2 * pair + ii].rearrange("m u p e -> m (u p e)").bitcast(F32)
+        def turn_b(b, first_bank, copies):
+            b_bf[b] = held([P, S2, 4], BF16, f"b_bf{b}")
+            for pair, copy in enumerate(copies):
+                turned = bank(first_bank + pair)
+                for n in range(2):
+                    words = b_abs[b][:, 2 * pair + n].rearrange("m u p e -> m (u p e)").bitcast(F32)
                     for u in range(2):
-                        nc.tensor.transpose(
-                            turned[:, Q * u + P * ii : Q * u + P * (ii + 1)], words[:, P * u : P * (u + 1)], ident[:]
-                        )
-                (nc.vector.tensor_copy if (b, pair) == (1, 0) else nc.scalar.copy)(
-                    g[:, Q * pair : Q * (pair + 1), :].rearrange("p m t -> p (m t)").bitcast(F32).rearrange("p (m u) -> p m u", u=2),
-                    turned[:].rearrange("p (u m) -> p m u", u=2),
-                )
+                        at = 2 * P * u + P * n
+                        nc.tensor.transpose(turned[:, at : at + P], words[:, P * u : P * (u + 1)], ident[:])
+                columns = b_bf[b][:, 2 * P * pair : 2 * P * (pair + 1), :].rearrange("p m t -> p (m t)").bitcast(F32)
+                copy(columns.rearrange("p (m u) -> p m u", u=2), turned[:].rearrange("p (u m) -> p m u", u=2))
 
-        def quant_b(b):
+        def quantise_b(b):
             b_c[b] = held([P, S2], U32, f"b_c{b}")
             b_s[b] = held([P, S2], U8, f"b_s{b}")
-            nc.vector.quantize_mx(b_c[b][:].bitcast(FP8X4), b_s[b][:], b_g[b][:].rearrange("p m t -> p (m t)"))
+            nc.vector.quantize_mx(b_c[b][:].bitcast(FP8X4), b_s[b][:], b_bf[b][:].rearrange("p m t -> p (m t)"))
 
-        h_c = {(b, h): held([P, BANK], U32, f"h_c{b}{h}") for b in range(PASSES) for h in range(2)}
-        h_s = {(b, h): held([P, BANK], U8, f"h_s{b}{h}") for b in range(PASSES) for h in range(2)}
-        th = {}
-        h_g = {}
+        h_c = {(b, half): held([P, BANK], U32, f"h_c{b}{half}") for b in range(PASSES) for half in range(2)}
+        h_s = {(b, half): held([P, BANK], U8, f"h_s{b}{half}") for b in range(PASSES) for half in range(2)}
+        tanh_f = {}
+        h_bf = {}
+        quarters = [slice(QUARTER * q, QUARTER * (q + 1)) for q in range(2)]
 
-        def state(b, h, first):
-            th[b, h] = held([P, 2, BANK, 2], F32, f"th{b}{h}")
-            h_g[b, h] = held([P, BANK, 2, 2], BF16, f"h_g{b}{h}")
-            for q in range(2):
-                cols = slice(Q * q, Q * (q + 1))
+        def tanh_state(b, half):
+            tanh_f[b, half] = held([P, 2, BANK, 2], F32, f"tanh_f{b}{half}")
+            h_bf[b, half] = held([P, BANK, 2, 2], BF16, f"h_bf{b}{half}")
+            for q, cols in enumerate(quarters):
                 for u in range(2):
-                    lin = bank(first + 2 * q + u)
+                    lin = bank(2 * q + u)
                     for e in range(2):
                         t = 2 * u + e
                         for a in range(PASSES):
                             nc.tensor.matmul_mx(
-                                lin[:, Q * e : Q * (e + 1)],
+                                lin[:, QUARTER * e : QUARTER * (e + 1)],
                                 lhsT=w1_c[b, a][:, P * t : P * (t + 1)].bitcast(FP8X4),
                                 lhsT_scale=w1_s[b, a][:, P * t : P * (t + 1)],
-                                rhs=v_w[a, h][:, cols].bitcast(FP8X4),
-                                rhs_scale=v_s[h][4 * a : P, cols],
+                                rhs=v_w[a, half][:, cols].bitcast(FP8X4),
+                                rhs_scale=v_s[half][4 * a : P, cols],
                                 start=(a == 0),
                                 stop=(a == PASSES - 1),
                             )
-                    nc.scalar.activation(th[b, h][:, u, cols, :], lin[:].rearrange("p (e n) -> p n e", e=2), ACT.Tanh)
+                    nc.scalar.activation(
+                        tanh_f[b, half][:, u, cols, :], lin[:].rearrange("p (e n) -> p n e", e=2), ACT.Tanh
+                    )
 
-        def gain_h(b, h, lo=0, hi=BANK):
-            nc.vector.tensor_tensor(
-                h_g[b, h][:, lo:hi],
-                th[b, h][:, :, lo:hi, :].rearrange("p u n e -> p n u e"),
-                gain_t[:, b : b + 1, :].rearrange("p o (u e) -> p o u e", u=2).to_broadcast([P, hi - lo, 2, 2]),
-                ALU.mult,
-            )
+        def apply_gain(b, half):
+            factors = gain_t[:, b : b + 1, :].rearrange("p o (u e) -> p o u e", u=2)
+            for cols in quarters:
+                nc.vector.tensor_tensor(
+                    h_bf[b, half][:, cols],
+                    tanh_f[b, half][:, :, cols, :].rearrange("p u n e -> p n u e"),
+                    factors.to_broadcast([P, QUARTER, 2, 2]),
+                    ALU.mult,
+                )
 
-        def quant_h(b, h, lo=0, hi=BANK):
-            nc.vector.quantize_mx(
-                h_c[b, h][:, lo:hi].bitcast(FP8X4),
-                h_s[b, h][:, lo:hi],
-                h_g[b, h][:, lo:hi].rearrange("p n u e -> p (n u e)"),
-            )
+        def quantise_h(b, half):
+            for cols in quarters:
+                nc.vector.quantize_mx(
+                    h_c[b, half][:, cols].bitcast(FP8X4),
+                    h_s[b, half][:, cols],
+                    h_bf[b, half][:, cols].rearrange("p n u e -> p (n u e)"),
+                )
 
-        lows = {}
+        lower = {}
 
-        def match(h, i, lo, hi, first):
-            ms = slice(P * i, P * (i + 1))
-            e2 = bank(first)
-            e1 = bank(first + 1)
+        def match(piece, first_bank):
+            half, i, lo, hi = piece
+            rows = slice(P * i, P * (i + 1))
+            e2 = bank(first_bank)
+            e1 = bank(first_bank + 1)
             width = hi - lo
             for acc, codes, planes in ((e2, b_c, b_s), (e1, v2_w, v2_planes)):
                 for b in range(PASSES):
                     nc.tensor.matmul_mx(
                         acc[:, :width],
-                        lhsT=codes[b][:, ms].bitcast(FP8X4),
-                        lhsT_scale=planes[b][:, ms],
-                        rhs=h_c[b, h][:, lo:hi].bitcast(FP8X4),
-                        rhs_scale=h_s[b, h][:, lo:hi],
+                        lhsT=codes[b][:, rows].bitcast(FP8X4),
+                        lhsT_scale=planes[b][:, rows],
+                        rhs=h_c[b, half][:, lo:hi].bitcast(FP8X4),
+                        rhs_scale=h_s[b, half][:, lo:hi],
                         start=(b == 0),
                         stop=(b == PASSES - 1),
                     )
@@ -252,61 +245,63 @@ def tile_list_opposite_blade_match_kernel(
             nc.scalar.copy(e2_sb[:, :width], e2[:, :width])
             low = ring.tile([P, BANK], F32, name="low")
             nc.vector.tensor_tensor(low[:, :width], e1[:, :width], e2_sb[:, :width], ALU.min)
-            lows[h, i, lo] = low
+            lower[piece] = low
 
-        def finish(h, i, lo, hi):
-            low = lows[h, i, lo]
-            res = ring.tile([P, BANK], F32, name="res")
+        def finish(piece):
+            half, i, lo, hi = piece
             width = hi - lo
-            if 4 * h + i < 2:
+            low = lower[piece]
+            res = ring.tile([P, BANK], F32, name="res")
+            if 4 * half + i < SCALAR_SEAT_TILES:
                 nc.scalar.activation(res[:, :width], low[:, :width], ACT.Copy, scale=seat_t[:, i : i + 1])
-            elif 4 * h + i < 6:
-                nc.gpsimd.tensor_scalar(res[:, :width], low[:, :width], seat_t[:, i : i + 1], 0.0, ALU.mult, ALU.add)
             else:
                 nc.vector.tensor_scalar_mul(res[:, :width], low[:, :width], seat_t[:, i : i + 1])
-            nc.sync.dma_start(out[P * i : P * (i + 1), BANK * h + lo : BANK * h + hi], res[:, :width])
+            nc.sync.dma_start(out[P * i : P * (i + 1), BANK * half + lo : BANK * half + hi], res[:, :width])
 
         project(0)
-        cast_w1(0, 0, "stage_a")
-        load_w1(1, 0, "slot_b")
-        load_w1(1, 1, "slot_s")
-        quant_w1(0, 0)
-        cast_w1(0, 1, "stage_b")
-        gain_t = held([P, PASSES, 4], F32, "gain_t", "slot_c")
+        round_w1(0, 0, nc.scalar.copy, "buf_bf_a")
+        load_w1(1, 0, "buf_w1_00")
+        load_w1(1, 1, "buf_tab_s")
+        quantise_w1(0, 0)
+        round_w1(0, 1, nc.scalar.copy, "buf_bf_b")
+        gain_t = held([P, PASSES, 4], F32, "gain_t", "buf_w1_01")
         nc.sync.dma_start(gain_t[:], gain.rearrange("(b p t) -> p b t", b=PASSES, t=4))
-        quant_w1(0, 1)
-        gather_second()
-        seat_t = held([P, S2 // P], F32, "seat_t", "slot_d")
+        quantise_w1(0, 1)
+        gather_pass1()
+        seat_t = placed([P, S2 // P], F32, "seat_t", S2 + S)
         with nc.allow_non_contiguous_dma(reason="one seat factor for each output row"):
             nc.sync.dma_start(seat_t[:], seat.rearrange("(i p) -> p i", p=P))
         project(1)
+
         abs_b(0, None)
-        state(0, 0, 0)
-        cast_w1(1, 0, "stage_b")
-        cast_w1(1, 1, "stage_a")
-        quant_w1(1, 0)
-        quant_w1(1, 1)
-        gain_h(0, 0)
-        state(1, 0, 0)
-        abs_b(1, "slot_b")
-        quant_h(0, 0)
-        turn_b(0, 4)
-        gain_h(1, 0)
-        turn_b(1, 6)
-        state(0, 1, 0)
-        quant_b(0)
-        quant_h(1, 0)
-        quant_b(1)
-        gain_h(0, 1)
-        state(1, 1, 0)
-        match(0, 0, 0, BANK, 4)
-        quant_h(0, 1)
-        gain_h(1, 1)
-        finish(0, 0, 0, BANK)
-        quant_h(1, 1)
-        pieces = [(h, i, 0, BANK) for h in range(2) for i in range(4)][:-1] + [(1, 3, 0, Q), (1, 3, Q, BANK)]
-        for n in range(1, len(pieces)):
-            match(*pieces[n], 4 + 2 * n)
-            if n > 1:
-                finish(*pieces[n - 1])
-        finish(*pieces[-1])
+        tanh_state(0, 0)
+        round_w1(1, 0, nc.vector.tensor_copy, "buf_bf_b")
+        round_w1(1, 1, nc.vector.tensor_copy, "buf_bf_a")
+        quantise_w1(1, 0)
+        quantise_w1(1, 1)
+        apply_gain(0, 0)
+        tanh_state(1, 0)
+        abs_b(1, "buf_w1_00")
+        quantise_h(0, 0)
+        turn_b(0, 4, (nc.scalar.copy, nc.scalar.copy))
+        apply_gain(1, 0)
+        turn_b(1, 6, (nc.vector.tensor_copy, nc.scalar.copy))
+        tanh_state(0, 1)
+        quantise_b(0)
+        quantise_h(1, 0)
+        quantise_b(1)
+        apply_gain(0, 1)
+        tanh_state(1, 1)
+
+        pieces = [(half, i, 0, BANK) for half in range(2) for i in range(4)][:-1]
+        pieces = pieces + [(1, 3, 0, QUARTER), (1, 3, QUARTER, BANK)]
+        match(pieces[0], 4)
+        quantise_h(0, 1)
+        apply_gain(1, 1)
+        finish(pieces[0])
+        quantise_h(1, 1)
+        match(pieces[1], 6)
+        for n in range(2, len(pieces)):
+            match(pieces[n], 4 + 2 * n)
+            finish(pieces[n - 1])
+        finish(pieces[-1])

from contextlib import ExitStack

import concourse.mybir as mybir
from concourse.masks import make_identity

K, T, S, S2 = 1024, 2048, 1024, 512
FLOPS = 2 * K * K * S + 2 * K * K * S2 + 4 * K * S * S2

F32 = mybir.dt.float32
BF16 = mybir.dt.bfloat16
I32 = mybir.dt.int32
U32 = mybir.dt.uint32
U16 = mybir.dt.uint16
U8 = mybir.dt.uint8
FP8X4 = mybir.dt.float8_e4m3fn_x4
FP4X4 = mybir.dt.float4_e2m1fn_x4
ACT = mybir.ActivationFunctionType
ALU = mybir.AluOpType

P = 128
K_PASS = 512
PASSES = K // K_PASS
BANK = 512
QUARTER = 256
PSUM_BANKS = 8
OUT_PIECES = 9
SCALAR_SEAT_TILES = 6


def tile_list_opposite_blade_match_kernel(
    tc, tab_words, tab_scales, offs, offs2, w1, gain, w4_words, w4_scales, seat, out
):
    nc = tc.nc
    with ExitStack() as ctx:
        keep = ctx.enter_context(tc.tile_pool(name="keep", bufs=1))
        table = ctx.enter_context(tc.tile_pool(name="table", bufs=1))
        ring = ctx.enter_context(tc.tile_pool(name="ring", bufs=OUT_PIECES))
        psum = ctx.enter_context(tc.psum_pool(name="psum", bufs=1))

        def held(shape, dtype, name, buffer=None):
            return keep.tile(shape, dtype, name=name, tag=buffer or name, align_bytes=64)

        def placed(shape, dtype, name, first_byte):
            return table.tile(shape, dtype, name=name, align_bytes=64, offset=first_byte)

        def bank(n):
            return psum.tile([P, BANK], F32, name=f"bank{n % PSUM_BANKS}")

        list2 = keep.tile([P, S2 // 16], U16, name="list2")
        list1 = keep.tile([P, S // 16], U16, name="list1")
        nc.sync.dma_start(list2[:], offs2)
        nc.sync.dma_start(list1[:], offs)

        tab_s = held([P, T], U8, "tab_s", "buf_tab_s")
        w4_s = held([P, PASSES, K], U8, "w4_s")
        nc.vector.memset(tab_s[:].bitcast(I32), 0)
        nc.gpsimd.memset(w4_s[:].bitcast(I32), 0)
        for quad in range(4):
            nc.scalar.dma_start(
                tab_s[32 * quad : 32 * quad + 8, :].bitcast(I32),
                tab_scales[:, 4 * quad : 4 * quad + 4, :].bitcast(I32),
            )
        for quad in range(4):
            nc.gpsimd.dma_start(
                w4_s[32 * quad : 32 * quad + 4, :, :].bitcast(I32),
                w4_scales[:, 4 * quad : 4 * quad + 4, :].rearrange("a q n -> q a n").bitcast(I32),
            )
        ident = held([P, P], F32, "ident")
        make_identity(nc, ident[:])

        tab_w = {}
        w1_raw = {}

        def load_table(a, first_byte):
            tab_w[a] = placed([P, T], U32, f"tab_w{a}", first_byte)
            nc.sync.dma_start(tab_w[a][:].bitcast(I32), tab_words[a].rearrange("p n t -> p (n t)").bitcast(I32))

        def load_w1(b, a, buffer):
            w1_raw[b, a] = held([P, 4, K_PASS], F32, f"w1_raw{b}{a}", buffer)
            nc.sync.dma_start(
                w1_raw[b, a][:],
                w1[K_PASS * a : K_PASS * (a + 1), K_PASS * b : K_PASS * (b + 1)].rearrange("(p j) c -> p j c", j=4),
            )

        load_table(0, 0)
        w4_w = held([P, PASSES, 2 * K], U8, "w4_w")
        nc.sync.dma_start(w4_w[:].bitcast(I32), w4_words.rearrange("a p n -> p a n").bitcast(I32))
        load_w1(0, 0, "buf_w1_00")
        load_w1(0, 1, "buf_w1_01")

        v2_w = [held([P, S2], U32, f"v2_w{a}") for a in range(PASSES)]
        v_w0 = held([P, S], U32, "v_w0")
        v_w1 = [held([P, BANK], U32, f"v_w1{half}") for half in range(2)]
        v_w = {(0, half): v_w0[:, BANK * half : BANK * (half + 1)] for half in range(2)}
        for half in range(2):
            v_w[1, half] = v_w1[half][:]

        v2_s1 = held([P, S2], U8, "v2_s1")
        nc.vector.memset(v2_s1[:].bitcast(I32), 0)
        nc.vector.tensor_copy(v2_w[0][:], tab_w[0][:].indirect(list2[:]))
        nc.vector.tensor_copy(v_w0[:], tab_w[0][:].indirect(list1[:]))
        load_table(1, S2 + S)
        picked_s = placed([P, S2 + S], U8, "picked_s", 0)
        v2_s = picked_s[:, :S2]
        v_s = [picked_s[:, S2 + BANK * half : S2 + BANK * (half + 1)] for half in range(2)]
        nc.vector.tensor_copy(v2_s, tab_s[:].indirect(list2[:]))
        nc.sync.dma_start(v2_s1[0 : P - 4, :].bitcast(I32), v2_s[4:P, :].bitcast(I32))
        v2_planes = [v2_s, v2_s1[:]]
        nc.vector.tensor_copy(picked_s[:, S2:], tab_s[:].indirect(list1[:]))

        def gather_pass1():
            nc.vector.tensor_copy(v2_w[1][:], tab_w[1][:].indirect(list2[:]))
            for half in range(2):
                entries = list1[:, BANK // 16 * half : BANK // 16 * (half + 1)]
                nc.vector.tensor_copy(v_w1[half][:], tab_w[1][:].indirect(entries))

        w1_bf = {}
        w1_c = {}
        w1_s = {}

        def round_w1(b, a, copy, buffer):
            w1_bf[b, a] = held([P, 4, P, 4], BF16, f"w1_bf{b}{a}", buffer)
            copy(w1_bf[b, a][:].rearrange("p t n j -> p n t j"), w1_raw[b, a][:].rearrange("p j (n t) -> p n t j", t=4))

        def quantise_w1(b, a):
            w1_c[b, a] = held([P, K_PASS], U32, f"w1_c{b}{a}")
            w1_s[b, a] = held([P, K_PASS], U8, f"w1_s{b}{a}")
            nc.vector.quantize_mx(
                w1_c[b, a][:].bitcast(FP8X4), w1_s[b, a][:], w1_bf[b, a][:].rearrange("p t n j -> p (t n j)")
            )

        proj = {}

        def project(a):
            for b in range(PASSES):
                for i in range(4):
                    if a == 0:
                        proj[b, i] = bank(4 * b + i)
                    nc.tensor.matmul_mx(
                        proj[b, i][:],
                        lhsT=v2_w[a][:, P * i : P * (i + 1)].bitcast(FP8X4),
                        lhsT_scale=v2_planes[a][:, P * i : P * (i + 1)],
                        rhs=w4_w[:, a, 2 * K_PASS * b : 2 * K_PASS * (b + 1)].bitcast(FP4X4),
                        rhs_scale=w4_s[:, a, K_PASS * b : K_PASS * (b + 1)],
                        start=(a == 0),
                        stop=(a == PASSES - 1),
                    )

        b_abs = {}

        def abs_b(b, buffer):
            b_abs[b] = held([P, 4, 2, P, 2], BF16, f"b_abs{b}", buffer)
            for i in range(4):
                nc.scalar.activation(
                    b_abs[b][:, i], proj[b, i][:].rearrange("m (p u e) -> m u p e", u=2, e=2), ACT.Abs
                )

        b_bf = {}
        b_c = {}
        b_s = {}

        def turn_b(b, first_bank, copies):
            b_bf[b] = held([P, S2, 4], BF16, f"b_bf{b}")
            for pair, copy in enumerate(copies):
                turned = bank(first_bank + pair)
                for n in range(2):
                    words = b_abs[b][:, 2 * pair + n].rearrange("m u p e -> m (u p e)").bitcast(F32)
                    for u in range(2):
                        at = 2 * P * u + P * n
                        nc.tensor.transpose(turned[:, at : at + P], words[:, P * u : P * (u + 1)], ident[:])
                columns = b_bf[b][:, 2 * P * pair : 2 * P * (pair + 1), :].rearrange("p m t -> p (m t)").bitcast(F32)
                copy(columns.rearrange("p (m u) -> p m u", u=2), turned[:].rearrange("p (u m) -> p m u", u=2))

        def quantise_b(b):
            b_c[b] = held([P, S2], U32, f"b_c{b}")
            b_s[b] = held([P, S2], U8, f"b_s{b}")
            nc.vector.quantize_mx(b_c[b][:].bitcast(FP8X4), b_s[b][:], b_bf[b][:].rearrange("p m t -> p (m t)"))

        h_c = {(b, half): held([P, BANK], U32, f"h_c{b}{half}") for b in range(PASSES) for half in range(2)}
        h_s = {(b, half): held([P, BANK], U8, f"h_s{b}{half}") for b in range(PASSES) for half in range(2)}
        tanh_f = {}
        h_bf = {}
        quarters = [slice(QUARTER * q, QUARTER * (q + 1)) for q in range(2)]

        def tanh_state(b, half):
            tanh_f[b, half] = held([P, 2, BANK, 2], F32, f"tanh_f{b}{half}")
            h_bf[b, half] = held([P, BANK, 2, 2], BF16, f"h_bf{b}{half}")
            for q, cols in enumerate(quarters):
                for u in range(2):
                    lin = bank(2 * q + u)
                    for e in range(2):
                        t = 2 * u + e
                        for a in range(PASSES):
                            nc.tensor.matmul_mx(
                                lin[:, QUARTER * e : QUARTER * (e + 1)],
                                lhsT=w1_c[b, a][:, P * t : P * (t + 1)].bitcast(FP8X4),
                                lhsT_scale=w1_s[b, a][:, P * t : P * (t + 1)],
                                rhs=v_w[a, half][:, cols].bitcast(FP8X4),
                                rhs_scale=v_s[half][4 * a : P, cols],
                                start=(a == 0),
                                stop=(a == PASSES - 1),
                            )
                    nc.scalar.activation(
                        tanh_f[b, half][:, u, cols, :], lin[:].rearrange("p (e n) -> p n e", e=2), ACT.Tanh
                    )

        def apply_gain(b, half):
            factors = gain_t[:, b : b + 1, :].rearrange("p o (u e) -> p o u e", u=2)
            for cols in quarters:
                nc.vector.tensor_tensor(
                    h_bf[b, half][:, cols],
                    tanh_f[b, half][:, :, cols, :].rearrange("p u n e -> p n u e"),
                    factors.to_broadcast([P, QUARTER, 2, 2]),
                    ALU.mult,
                )

        def quantise_h(b, half):
            for cols in quarters:
                nc.vector.quantize_mx(
                    h_c[b, half][:, cols].bitcast(FP8X4),
                    h_s[b, half][:, cols],
                    h_bf[b, half][:, cols].rearrange("p n u e -> p (n u e)"),
                )

        lower = {}

        def match(piece, first_bank):
            half, i, lo, hi = piece
            rows = slice(P * i, P * (i + 1))
            e2 = bank(first_bank)
            e1 = bank(first_bank + 1)
            width = hi - lo
            for acc, codes, planes in ((e2, b_c, b_s), (e1, v2_w, v2_planes)):
                for b in range(PASSES):
                    nc.tensor.matmul_mx(
                        acc[:, :width],
                        lhsT=codes[b][:, rows].bitcast(FP8X4),
                        lhsT_scale=planes[b][:, rows],
                        rhs=h_c[b, half][:, lo:hi].bitcast(FP8X4),
                        rhs_scale=h_s[b, half][:, lo:hi],
                        start=(b == 0),
                        stop=(b == PASSES - 1),
                    )
            e2_sb = ring.tile([P, BANK], F32, name="e2_sb")
            nc.scalar.copy(e2_sb[:, :width], e2[:, :width])
            low = ring.tile([P, BANK], F32, name="low")
            nc.vector.tensor_tensor(low[:, :width], e1[:, :width], e2_sb[:, :width], ALU.min)
            lower[piece] = low

        def finish(piece):
            half, i, lo, hi = piece
            width = hi - lo
            low = lower[piece]
            res = ring.tile([P, BANK], F32, name="res")
            if 4 * half + i < SCALAR_SEAT_TILES:
                nc.scalar.activation(res[:, :width], low[:, :width], ACT.Copy, scale=seat_t[:, i : i + 1])
            else:
                nc.vector.tensor_scalar_mul(res[:, :width], low[:, :width], seat_t[:, i : i + 1])
            nc.sync.dma_start(out[P * i : P * (i + 1), BANK * half + lo : BANK * half + hi], res[:, :width])

        project(0)
        round_w1(0, 0, nc.scalar.copy, "buf_bf_a")
        load_w1(1, 0, "buf_w1_00")
        load_w1(1, 1, "buf_tab_s")
        quantise_w1(0, 0)
        round_w1(0, 1, nc.scalar.copy, "buf_bf_b")
        gain_t = held([P, PASSES, 4], F32, "gain_t", "buf_w1_01")
        nc.sync.dma_start(gain_t[:], gain.rearrange("(b p t) -> p b t", b=PASSES, t=4))
        quantise_w1(0, 1)
        gather_pass1()
        seat_t = placed([P, S2 // P], F32, "seat_t", S2 + S)
        with nc.allow_non_contiguous_dma(reason="one seat factor for each output row"):
            nc.sync.dma_start(seat_t[:], seat.rearrange("(i p) -> p i", p=P))
        project(1)

        abs_b(0, None)
        tanh_state(0, 0)
        round_w1(1, 0, nc.vector.tensor_copy, "buf_bf_b")
        round_w1(1, 1, nc.vector.tensor_copy, "buf_bf_a")
        quantise_w1(1, 0)
        quantise_w1(1, 1)
        apply_gain(0, 0)
        tanh_state(1, 0)
        abs_b(1, "buf_w1_00")
        quantise_h(0, 0)
        turn_b(0, 4, (nc.scalar.copy, nc.scalar.copy))
        apply_gain(1, 0)
        turn_b(1, 6, (nc.vector.tensor_copy, nc.scalar.copy))
        tanh_state(0, 1)
        quantise_b(0)
        quantise_h(1, 0)
        quantise_b(1)
        apply_gain(0, 1)
        tanh_state(1, 1)

        pieces = [(half, i, 0, BANK) for half in range(2) for i in range(4)][:-1]
        pieces = pieces + [(1, 3, 0, QUARTER), (1, 3, QUARTER, BANK)]
        match(pieces[0], 4)
        quantise_h(0, 1)
        apply_gain(1, 1)
        finish(pieces[0])
        quantise_h(1, 1)
        match(pieces[1], 6)
        for n in range(2, len(pieces)):
            match(pieces[n], 4 + 2 * n)
            finish(pieces[n - 1])
        finish(pieces[-1])
